import numpy as np
import ml_dtypes


def mxq(x, axis, fmt="e4m3"):
    dtype, down = {"e4m3": (ml_dtypes.float8_e4m3fn, 7), "e5m2": (ml_dtypes.float8_e5m2, 14)}[fmt]
    v = np.moveaxis(np.asarray(x, np.float32).astype(ml_dtypes.bfloat16).astype(np.float64), axis, -1)
    blocks = v.reshape(v.shape[:-1] + (-1, 32))
    amax = np.abs(blocks).max(-1, keepdims=True)
    byte = np.maximum(np.where(amax > 0, np.frexp(amax)[1] - 1 + 127, 0) - down, 1)
    scale = np.exp2(byte - 127.0)
    codes = (blocks / scale).astype(np.float32).astype(dtype).astype(np.float64)
    return np.moveaxis((codes * scale).reshape(v.shape), -1, axis)


WIDE = False


def mx_kscale(k):
    if not WIDE:
        return np.ones(k)
    levels = np.array([10, -10, 5, -5, 0])
    if k % 512:
        return np.exp2(np.random.permutation(np.resize(levels, k // 32))).repeat(32)
    a = np.empty((k // 512, 16))
    for p in range(k // 512):
        a[p, :8] = np.random.permutation(np.resize(levels, 8))
        for g in range(8):
            far = levels[np.abs(levels - a[p, g]) >= 10]
            a[p, g + 8] = far[np.random.randint(len(far))]
    return np.exp2(a.ravel()).repeat(32)


def f64(x):
    return np.asarray(x).astype(np.float64)


def striped(idx):
    return np.tile(idx.reshape(-1, 16).T, (8, 1)).astype(np.uint16)


def unstriped(offs):
    return offs[:16].T.reshape(-1).astype(np.int64)


E2M1 = np.array([0.0, 0.5, 1.0, 1.5, 2.0, 3.0, 4.0, 6.0, -0.0, -0.5, -1.0, -1.5, -2.0, -3.0, -4.0, -6.0])


def pack_weight(w, fmt):
    k, n = w.shape
    w = f64(np.asarray(w, np.float32).astype(ml_dtypes.bfloat16)).reshape(k // 32, 32, n)
    amax = np.abs(w).max(1)
    if fmt == "e4m3":
        byte = np.frexp(amax)[1] - 1 + 127 - 7
    else:
        mant, ex = np.frexp(amax / 6.0)
        byte = np.where(mant > 0.5, ex, ex - 1) + 127
    byte = np.clip(np.where(amax > 0, byte, 1), 1, 254)
    scaled = (w * np.exp2(127.0 - byte)[:, None, :]).reshape(k, n).astype(np.float32)
    by_word = np.ascontiguousarray(scaled.reshape(k // 512, 128, 4, n).transpose(0, 1, 3, 2))
    if fmt == "e4m3":
        words = by_word.astype(ml_dtypes.float8_e4m3fn).view(np.uint8)
    else:
        c = by_word.astype(ml_dtypes.float4_e2m1fn).view(np.uint8) & 0xF
        words = (c[..., 0::2] | (c[..., 1::2] << 4)).reshape(k // 512, 128, 2 * n)
    return np.ascontiguousarray(words), np.ascontiguousarray(byte.astype(np.uint8).reshape(k // 512, 16, n))


def unpack_weight(words, scales, fmt):
    g, _, n = scales.shape
    words = np.ascontiguousarray(words).reshape(g, 128, n, -1)
    if fmt == "e4m3":
        vals = words.view(ml_dtypes.float8_e4m3fn).astype(np.float64)
    else:
        nib = np.empty((g, 128, n, 4), np.uint8)
        nib[..., 0::2] = words & 0xF
        nib[..., 1::2] = words >> 4
        vals = E2M1[nib]
    vals = vals * np.repeat(np.exp2(scales.astype(np.float64) - 127.0), 8, axis=1)[..., None]
    return vals.transpose(0, 1, 3, 2).reshape(g * 512, n)


def gelu(v):
    return 0.5 * v * (1.0 + np.tanh(np.sqrt(2.0 / np.pi) * (v + 0.044715 * v**3)))


def bf(x):
    return np.asarray(x, np.float32).astype(ml_dtypes.bfloat16)


def planes(Y):
    n, m = Y.shape
    b = f64(bf(Y)).reshape(n // 32, 32, m)
    amax = np.abs(b).max(1)
    byte = np.clip(np.where(amax > 0, np.frexp(amax)[1] - 1 + 127 - 7, 1), 1, 254)
    codes = (b * np.exp2(127.0 - byte)[:, None, :]).reshape(n, m).astype(np.float32).astype(ml_dtypes.float8_e4m3fn).view(np.uint8)
    words = codes.reshape(n // 512, 128, 4, m).transpose(0, 1, 3, 2)
    return np.ascontiguousarray(words), np.ascontiguousarray(byte.astype(np.uint8).reshape(n // 512, 16, m))


K, T, S, H, P, N = 2048, 2048, 1024, 512, 512, 1024

def setup_inputs():
    n = np.random.standard_normal
    s = mx_kscale(K)[:, None]
    u = mx_kscale(H)[:, None]
    size = np.exp(0.8 * n(N))
    tab_words, tab_scales = pack_weight(n((K, T)) * s, "e4m3")
    w2_words, w2_scales = pack_weight(n((H, N)) / np.sqrt(H) / u * size, "e2m1")
    return {
        "tab_words": tab_words, "tab_scales": tab_scales,
        "offs": striped(np.random.permutation(T)[:S]),
        "pos1": striped(np.random.permutation(S)[:P]),
        "pos2": striped(np.random.permutation(S)[:P]),
        "w1": (0.72 * n((K, H)) / np.sqrt(K) / s).astype(np.float32),
        "w2_words": w2_words, "w2_scales": w2_scales,
        "temp": np.random.uniform(0.4, 1.6, H).astype(np.float32),
        "lean": (np.where(n(H) > 0, 1.0, -1.0) * np.random.uniform(1.5, 4.0, H)).astype(np.float32),
        "rate": np.random.uniform(0.58, 0.82, H).astype(np.float32),
        "gain": (np.random.uniform(0.6, 1.8, H) * u[:, 0]).astype(np.float32),
        "base": (0.5 * n(N) * size).astype(np.float32),
    }

def reference(tab_words, tab_scales, offs, pos1, pos2, w1, w2_words, w2_scales, temp, lean, rate, gain, base):
    v = unpack_weight(tab_words, tab_scales, "e4m3")[:, unstriped(offs)]
    h = mxq(f64(w1), 0, "e4m3").T @ v
    top = h.max(axis=1)
    a = np.exp(f64(temp)[:, None] * (h[:, unstriped(pos1)] - top[:, None]))
    c = h[:, unstriped(pos2)]
    close = np.maximum(f64(lean)[:, None] * a, c)
    close = close + np.sin(f64(rate)[:, None] * c)
    z = mxq(f64(gain)[:, None] * close, 0, "e4m3")
    w2 = unpack_weight(w2_words, w2_scales, "e2m1")
    y = (w2.T @ z) + f64(base)[:, None]
    words, scales = planes(y)
    return y, words, scales

@@ -1,0 +1,280 @@
+import math
+from contextlib import ExitStack
+
+import concourse.mybir as mybir
+
+K, T, S, H, PAIRS, N = 2048, 2048, 1024, 512, 512, 1024
+FLOPS = 2 * K * H * S + 2 * H * N * PAIRS
+
+F32 = mybir.dt.float32
+BF16 = mybir.dt.bfloat16
+I32 = mybir.dt.int32
+U32 = mybir.dt.uint32
+U16 = mybir.dt.uint16
+U8 = mybir.dt.uint8
+FP8X4 = mybir.dt.float8_e4m3fn_x4
+FP4X4 = mybir.dt.float4_e2m1fn_x4
+ALU = mybir.AluOpType
+ACT = mybir.ActivationFunctionType
+
+P = 128
+PACK = 4
+K_PASS = P * PACK
+PASSES = K // K_PASS
+BANK = 512
+GROUPS = N // K_PASS
+HALF = PAIRS // 2
+LAST_VECTOR_COLUMNS = 48
+
+
+def tile_list_kinship_closeness_kernel(
+    tc, tab_words, tab_scales, offs, pos1, pos2, w1, w2_words, w2_scales, temp, lean, rate, gain, base, out_0, out_1, out_2
+):
+    nc = tc.nc
+    with ExitStack() as ctx:
+        keep = ctx.enter_context(tc.tile_pool(name="keep", bufs=1))
+        psum = ctx.enter_context(tc.psum_pool(name="psum", bufs=1))
+
+        def sb(shape, dtype, name):
+            return keep.tile(shape, dtype, name=name, align_bytes=64)
+
+        offs_sb = keep.tile([P, S // 16], U16, name="offs_sb")
+        pos1_sb = keep.tile([P, PAIRS // 16], U16, name="pos1_sb")
+        pos2_sb = keep.tile([P, PAIRS // 16], U16, name="pos2_sb")
+        tab = [sb([P, T], U32, f"tab{a}") for a in range(PASSES)]
+        raw = [sb([P, PACK, H], F32, f"raw{a}") for a in range(PASSES - 1)]
+        raw_last = [sb([P, PACK, H // 2], F32, f"raw_last{u}") for u in range(2)]
+        w2_in = sb([P, 2 * N], U8, "w2_in")
+
+        def w1_rows(a):
+            return w1[a * K_PASS : (a + 1) * K_PASS, :].rearrange("(p j) c -> p j c", j=PACK)
+
+        tab_sc = sb([P, T], U8, "tab_sc")
+        w2_sc_in = sb([P, N], U8, "w2_sc_in")
+        nc.vector.memset(tab_sc[:].bitcast(I32), 0)
+        nc.vector.memset(w2_sc_in[:].bitcast(I32), 0)
+        row = {name: sb([P, PACK], F32, name + "_sb") for name in ("temp", "lean", "rate", "gain")}
+        base_sb = sb([P, GROUPS, PACK], F32, "base_sb")
+        nc.sync.dma_start(offs_sb[:], offs)
+        for a in range(PASSES):
+            nc.sync.dma_start(out=tab[a][:].bitcast(I32), in_=tab_words[a].rearrange("p t i -> p (t i)").bitcast(I32))
+            if a == 0:
+                for q in range(4):
+                    nc.sync.dma_start(
+                        out=tab_sc[32 * q : 32 * q + 16, :].bitcast(I32), in_=tab_scales[:, 4 * q : 4 * q + 4, :].bitcast(I32)
+                    )
+            if a == 1:
+                for name, src in (("temp", temp), ("lean", lean), ("rate", rate), ("gain", gain)):
+                    nc.sync.dma_start(out=row[name][:], in_=src.rearrange("(p t) -> p t", t=PACK))
+                nc.sync.dma_start(out=base_sb[:], in_=base.rearrange("(g p t) -> p g t", g=GROUPS, t=PACK))
+            if a < PASSES - 1:
+                nc.sync.dma_start(out=raw[a][:], in_=w1_rows(a))
+            if a == 1:
+                for q in range(4):
+                    nc.sync.dma_start(
+                        out=w2_sc_in[32 * q : 32 * q + 4, :].bitcast(I32), in_=w2_scales[0, 4 * q : 4 * q + 4, :].bitcast(I32)
+                    )
+        for u in range(2):
+            nc.sync.dma_start(out=raw_last[u][:], in_=w1_rows(PASSES - 1)[:, :, u * (H // 2) : (u + 1) * (H // 2)])
+        nc.sync.dma_start(pos1_sb[:], pos1)
+        nc.sync.dma_start(pos2_sb[:], pos2)
+        nc.sync.dma_start(out=w2_in[:].bitcast(I32), in_=w2_words[0].bitcast(I32))
+
+        def small(name, width=PACK):
+            return sb([P, width], F32, name)
+
+        step, sign, size, size2, root, root2, neg_root = [small(n) for n in ("step", "sign", "size", "size2", "root", "root2", "neg_root")]
+        half_power, rate_quarter, turn, neg_temp = [small(n) for n in ("half_power", "rate_quarter", "turn", "neg_temp")]
+        one, shift = small("one", 1), small("shift", 1)
+        nc.gpsimd.memset(half_power[:], 0.5)
+        nc.gpsimd.memset(one[:], 1.0)
+        nc.gpsimd.tensor_scalar(shift[:], one[:], -math.pi / 8.0, 0.0, ALU.mult, ALU.add)
+        nc.gpsimd.tensor_scalar(neg_temp[:], row["temp"][:], -1.0, 0.0, ALU.mult, ALU.add)
+        nc.gpsimd.tensor_scalar(step[:], row["gain"][:], 0.0, None, ALU.is_ge)
+        nc.gpsimd.tensor_scalar(sign[:], step[:], 2.0, -1.0, ALU.mult, ALU.add)
+        nc.gpsimd.tensor_tensor(size[:], row["gain"][:], sign[:], ALU.mult)
+        nc.gpsimd.tensor_scalar(size2[:], size[:], 2.0, 0.0, ALU.mult, ALU.add)
+        nc.gpsimd.tensor_tensor(root[:], size2[:], half_power[:], ALU.pow)
+        nc.gpsimd.tensor_scalar(root2[:], root[:], 2.0, 0.0, ALU.mult, ALU.add)
+        nc.gpsimd.tensor_scalar(neg_root[:], root[:], -1.0, 0.0, ALU.mult, ALU.add)
+        nc.gpsimd.tensor_scalar(rate_quarter[:], row["rate"][:], 0.25, 0.0, ALU.mult, ALU.add)
+        nc.gpsimd.tensor_tensor(turn[:], rate_quarter[:], sign[:], ALU.mult)
+
+        w2_sc = sb([P, N], U8, "w2_sc")
+        nc.gpsimd.tensor_copy(
+            out=w2_sc[:].rearrange("p (g t q) -> p g t q", g=GROUPS, t=PACK),
+            in_=w2_sc_in[:].rearrange("p (g q t) -> p g t q", g=GROUPS, t=PACK),
+        )
+
+        v_words = [sb([P, S], U32, f"v_words{a}") for a in range(PASSES)]
+        v_sc = sb([P, S], U8, "v_sc")
+        w_bf = [sb([P, PACK, P, PACK], BF16, f"w_bf{a}") for a in range(PASSES)]
+        w_codes = [sb([P, H], U32, f"w_codes{a}") for a in range(PASSES)]
+        w_sc = [sb([P, H], U8, f"w_sc{a}") for a in range(PASSES)]
+        h_ps = [[psum.tile([P, BANK], F32, name=f"h_ps{t}{u}", tag=f"bank{2 * t + u}") for u in range(2)] for t in range(PACK)]
+
+        def dealt(a, src, m0, m1, first):
+            dst = w_bf[a][:, :, m0:m1, :].rearrange("p t m j -> p m j t")
+            view = src[:].rearrange("p j (m t) -> p m j t", t=PACK)[:, m0 - first : m1 - first, :, :]
+            return dst, view
+
+        def quantize_w(a, t0, t1):
+            nc.vector.quantize_mx(
+                out=w_codes[a][:, t0 * P : t1 * P].bitcast(FP8X4),
+                scales=w_sc[a][:, t0 * P : t1 * P],
+                in_=w_bf[a][:, t0:t1, :, :].rearrange("p t m j -> p (t m j)"),
+            )
+
+        def first_matmuls(a, t):
+            for u in range(2):
+                cols = slice(u * BANK, (u + 1) * BANK)
+                nc.tensor.matmul_mx(
+                    out=h_ps[t][u][:],
+                    lhsT=w_codes[a][:, t * P : (t + 1) * P].bitcast(FP8X4),
+                    lhsT_scale=w_sc[a][:, t * P : (t + 1) * P],
+                    rhs=v_words[a][:, cols].bitcast(FP8X4),
+                    rhs_scale=v_sc[4 * a : P, cols],
+                    start=(a == 0),
+                    stop=(a == PASSES - 1),
+                )
+
+        for a in range(PASSES):
+            nc.vector.tensor_copy(out=v_words[a][:], in_=tab[a][:].indirect(offs_sb[:]))
+            if a == 0:
+                nc.vector.tensor_copy(out=v_sc[:], in_=tab_sc[:].indirect(offs_sb[:]))
+            if a < PASSES - 1:
+                dst, view = dealt(a, raw[a], 0, P, 0)
+                nc.scalar.activation(out=dst, in_=view, func=ACT.Copy)
+                quantize_w(a, 0, PACK)
+                for t in range(PACK):
+                    first_matmuls(a, t)
+        last = PASSES - 1
+        mid = P // 2
+        cut = mid + LAST_VECTOR_COLUMNS
+        dst, view = dealt(last, raw_last[0], 0, mid, 0)
+        nc.scalar.activation(out=dst, in_=view, func=ACT.Copy)
+        dst, view = dealt(last, raw_last[1], mid, cut, mid)
+        nc.vector.tensor_copy(out=dst, in_=view)
+        dst, view = dealt(last, raw_last[1], cut, P, mid)
+        nc.scalar.activation(out=dst, in_=view, func=ACT.Copy)
+        for t in range(PACK):
+            quantize_w(last, t, t + 1)
+            first_matmuls(last, t)
+
+        w2_dealt = sb([P, 2 * N], U8, "w2_dealt")
+        nc.scalar.copy(
+            out=w2_dealt[:].bitcast(U16).rearrange("p (g t q) -> p g t q", g=GROUPS, t=PACK),
+            in_=w2_in[:].bitcast(U16).rearrange("p (g q t) -> p g t q", g=GROUPS, t=PACK),
+        )
+
+        h = [sb([P, S], F32, f"h{t}") for t in range(PACK)]
+        peak = [sb([P, 2], F32, f"peak{t}") for t in range(PACK)]
+        look_bias = sb([P, PACK], F32, "look_bias")
+        look = [sb([P, PAIRS], F32, f"look{t}") for t in range(PACK)]
+        pick = [sb([P, PAIRS], F32, f"pick{t}") for t in range(PACK)]
+        for t in range(PACK):
+            for u in range(2):
+                nc.vector.tensor_scalar(
+                    h[t][:, u * BANK : (u + 1) * BANK], h_ps[t][u][:], 1.0, None, ALU.mult, ALU.max, accum_out=peak[t][:, u : u + 1]
+                )
+            nc.gpsimd.tensor_scalar(
+                look_bias[:, t : t + 1], peak[t][:, 0:1], peak[t][:, 1:2], neg_temp[:, t : t + 1], ALU.max, ALU.mult
+            )
+            nc.scalar.activation(
+                out=look[t][:],
+                in_=h[t][:].indirect(pos1_sb[:]),
+                func=ACT.Exp,
+                bias=look_bias[:, t : t + 1],
+                scale=row["temp"][:, t : t + 1],
+            )
+        for t in range(PACK):
+            nc.vector.tensor_copy(out=pick[t][:], in_=h[t][:].indirect(pos2_sb[:]))
+        larger = look
+        gained = sb([P, PACK, PAIRS], F32, "gained")
+        for t in range(PACK):
+            nc.vector.scalar_tensor_tensor(larger[t][:], look[t][:], row["lean"][:, t : t + 1], pick[t][:], ALU.mult, ALU.max)
+        for t in range(PACK):
+            nc.vector.tensor_scalar(
+                gained[:, t, :], larger[t][:], row["gain"][:, t : t + 1], size[:, t : t + 1], ALU.mult, ALU.subtract
+            )
+
+        wave = [sb([P, PACK, HALF], F32, f"wave{u}") for u in range(2)]
+        for u in range(2):
+            cols = slice(u * HALF, (u + 1) * HALF)
+            sine = [sb([P, HALF], F32, f"sine{u}{t}") for t in range(PACK)]
+            square = [sb([P, HALF], F32, f"square{u}{t}") for t in range(PACK)]
+            for t in range(PACK):
+                nc.scalar.activation(out=sine[t][:], in_=pick[t][:, cols], func=ACT.Sin, scale=turn[:, t : t + 1], bias=shift[:])
+            for t in range(PACK):
+                nc.scalar.activation(out=square[t][:], in_=sine[t][:], func=ACT.Square)
+            for t in range(PACK):
+                nc.scalar.activation(
+                    out=wave[u][:, t, :], in_=square[t][:], func=ACT.Square, scale=root2[:, t : t + 1], bias=neg_root[:, t : t + 1]
+                )
+
+        z_codes = [sb([P, HALF], U32, f"z_codes{u}") for u in range(2)]
+        z_sc = [sb([P, HALF], U8, f"z_sc{u}") for u in range(2)]
+        y = [[sb([P, PACK, HALF], F32, f"y{u}{g}") for g in range(GROUPS)] for u in range(2)]
+        y_sc = sb([P, GROUPS, PAIRS], U8, "y_sc")
+
+        def make_z(u):
+            cols = slice(u * HALF, (u + 1) * HALF)
+            z_woven = sb([P, HALF, PACK], BF16, f"z_woven{u}")
+            nc.vector.tensor_tensor(
+                z_woven[:].rearrange("p (c i) t -> p c t i", i=4),
+                gained[:, :, cols].rearrange("p t (c i) -> p c t i", i=4),
+                wave[u][:].rearrange("p t (c i) -> p c t i", i=4),
+                ALU.add,
+            )
+            return z_woven
+
+        def second_stage(u, z_woven):
+            cols = slice(u * HALF, (u + 1) * HALF)
+            nc.vector.quantize_mx(out=z_codes[u][:].bitcast(FP8X4), scales=z_sc[u][:], in_=z_woven[:].rearrange("p m t -> p (m t)"))
+            for g in range(GROUPS):
+                for pair in range(2):
+                    bank = 4 * u + 2 * g + pair
+                    y_ps = psum.tile([P, 2, HALF], F32, name=f"y_ps{bank}", tag=f"bank{bank}")
+                    for e in range(2):
+                        col = (g * PACK + 2 * pair + e) * P
+                        nc.tensor.matmul_mx(
+                            out=y_ps[:, e, :],
+                            lhsT=w2_dealt[:, 2 * col : 2 * (col + P)].bitcast(FP4X4),
+                            lhsT_scale=w2_sc[:, col : col + P],
+                            rhs=z_codes[u][:].bitcast(FP8X4),
+                            rhs_scale=z_sc[u][:],
+                            start=True,
+                            stop=True,
+                        )
+                    for e in range(2):
+                        t = 2 * pair + e
+                        nc.scalar.activation(out=y[u][g][:, t, :], in_=y_ps[:, e, :], func=ACT.Identity, bias=base_sb[:, g, t : t + 1])
+                rows = out_0[g * K_PASS : (g + 1) * K_PASS, cols].rearrange("(p t) m -> p t m", t=PACK)
+                nc.sync.dma_start(out=rows, in_=y[u][g][:])
+
+        def planes(u):
+            cols = slice(u * HALF, (u + 1) * HALF)
+            for g in range(GROUPS):
+                y_woven = sb([P, HALF, PACK], BF16, f"y_woven{u}{g}")
+                y_codes = sb([P, HALF], U32, f"y_codes{u}{g}")
+                nc.vector.tensor_copy(
+                    out=y_woven[:].rearrange("p (c i) t -> p c t i", i=4), in_=y[u][g][:].rearrange("p t (c i) -> p c t i", i=4)
+                )
+                nc.vector.quantize_mx(
+                    out=y_codes[:].bitcast(FP8X4), scales=y_sc[:, g, cols], in_=y_woven[:].rearrange("p m t -> p (m t)")
+                )
+                nc.sync.dma_start(
+                    out=out_1[g, :, cols, :].rearrange("p m t -> p (m t)").bitcast(I32), in_=y_codes[:].bitcast(I32)
+                )
+
+        woven = [make_z(0)]
+        second_stage(0, woven[0])
+        woven.append(make_z(1))
+        second_stage(1, woven[1])
+        planes(0)
+        planes(1)
+        for q in range(4):
+            nc.sync.dma_start(
+                out=out_2[:, 4 * q : 4 * q + 4, :].rearrange("g r m -> r g m").bitcast(I32),
+                in_=y_sc[32 * q : 32 * q + 4, :, :].bitcast(I32),
+            )

@@ -24,6 +24,7 @@ PASSES = K // K_PASS
 BANK = 512
 GROUPS = N // K_PASS
 HALF = PAIRS // 2
+THIRD_VECTOR_COLUMNS = 56
 LAST_VECTOR_COLUMNS = 48
 
 
@@ -35,8 +36,8 @@ def tile_list_kinship_closeness_kernel(
         keep = ctx.enter_context(tc.tile_pool(name="keep", bufs=1))
         psum = ctx.enter_context(tc.psum_pool(name="psum", bufs=1))
 
-        def sb(shape, dtype, name):
-            return keep.tile(shape, dtype, name=name, align_bytes=64)
+        def sb(shape, dtype, name, tag=None):
+            return keep.tile(shape, dtype, name=name, tag=tag or name, align_bytes=64)
 
         offs_sb = keep.tile([P, S // 16], U16, name="offs_sb")
         pos1_sb = keep.tile([P, PAIRS // 16], U16, name="pos1_sb")
@@ -44,25 +45,24 @@ def tile_list_kinship_closeness_kernel(
         tab = [sb([P, T], U32, f"tab{a}") for a in range(PASSES)]
         raw = [sb([P, PACK, H], F32, f"raw{a}") for a in range(PASSES - 1)]
         raw_last = [sb([P, PACK, H // 2], F32, f"raw_last{u}") for u in range(2)]
-        w2_in = sb([P, 2 * N], U8, "w2_in")
+        w2_in = sb([P, 2 * N], U8, "w2_in", tag="look0")
 
         def w1_rows(a):
             return w1[a * K_PASS : (a + 1) * K_PASS, :].rearrange("(p j) c -> p j c", j=PACK)
 
         tab_sc = sb([P, T], U8, "tab_sc")
         w2_sc_in = sb([P, N], U8, "w2_sc_in")
-        nc.vector.memset(tab_sc[:].bitcast(I32), 0)
+        nc.gpsimd.memset(tab_sc[:].bitcast(I32), 0)
+        for q in range(4):
+            nc.gpsimd.dma_start(
+                out=tab_sc[32 * q : 32 * q + 16, :].bitcast(I32), in_=tab_scales[:, 4 * q : 4 * q + 4, :].bitcast(I32)
+            )
         nc.vector.memset(w2_sc_in[:].bitcast(I32), 0)
         row = {name: sb([P, PACK], F32, name + "_sb") for name in ("temp", "lean", "rate", "gain")}
         base_sb = sb([P, GROUPS, PACK], F32, "base_sb")
         nc.sync.dma_start(offs_sb[:], offs)
         for a in range(PASSES):
             nc.sync.dma_start(out=tab[a][:].bitcast(I32), in_=tab_words[a].rearrange("p t i -> p (t i)").bitcast(I32))
-            if a == 0:
-                for q in range(4):
-                    nc.sync.dma_start(
-                        out=tab_sc[32 * q : 32 * q + 16, :].bitcast(I32), in_=tab_scales[:, 4 * q : 4 * q + 4, :].bitcast(I32)
-                    )
             if a == 1:
                 for name, src in (("temp", temp), ("lean", lean), ("rate", rate), ("gain", gain)):
                     nc.sync.dma_start(out=row[name][:], in_=src.rearrange("(p t) -> p t", t=PACK))
@@ -143,8 +143,12 @@ def tile_list_kinship_closeness_kernel(
             if a == 0:
                 nc.vector.tensor_copy(out=v_sc[:], in_=tab_sc[:].indirect(offs_sb[:]))
             if a < PASSES - 1:
-                dst, view = dealt(a, raw[a], 0, P, 0)
+                share = THIRD_VECTOR_COLUMNS if a == 2 else 0
+                dst, view = dealt(a, raw[a], share, P, 0)
                 nc.scalar.activation(out=dst, in_=view, func=ACT.Copy)
+                if share:
+                    dst, view = dealt(a, raw[a], 0, share, 0)
+                    nc.vector.tensor_copy(out=dst, in_=view)
                 quantize_w(a, 0, PACK)
                 for t in range(PACK):
                     first_matmuls(a, t)
@@ -169,7 +173,7 @@ def tile_list_kinship_closeness_kernel(
 
         h = [sb([P, S], F32, f"h{t}") for t in range(PACK)]
         peak = [sb([P, 2], F32, f"peak{t}") for t in range(PACK)]
-        look_bias = sb([P, PACK], F32, "look_bias")
+        look_bias = sb([P, PACK], F32, "look_bias", tag="sine00")
         look = [sb([P, PAIRS], F32, f"look{t}") for t in range(PACK)]
         pick = [sb([P, PAIRS], F32, f"pick{t}") for t in range(PACK)]
         for t in range(PACK):
@@ -257,9 +261,7 @@ def tile_list_kinship_closeness_kernel(
             for g in range(GROUPS):
                 y_woven = sb([P, HALF, PACK], BF16, f"y_woven{u}{g}")
                 y_codes = sb([P, HALF], U32, f"y_codes{u}{g}")
-                nc.vector.tensor_copy(
-                    out=y_woven[:].rearrange("p (c i) t -> p c t i", i=4), in_=y[u][g][:].rearrange("p t (c i) -> p c t i", i=4)
-                )
+                nc.vector.tensor_copy(out=y_woven[:], in_=y[u][g][:].rearrange("p t m -> p m t"))
                 nc.vector.quantize_mx(
                     out=y_codes[:].bitcast(FP8X4), scales=y_sc[:, g, cols], in_=y_woven[:].rearrange("p m t -> p (m t)")
                 )

@@ -261,7 +261,9 @@ def tile_list_kinship_closeness_kernel(
             for g in range(GROUPS):
                 y_woven = sb([P, HALF, PACK], BF16, f"y_woven{u}{g}")
                 y_codes = sb([P, HALF], U32, f"y_codes{u}{g}")
-                nc.vector.tensor_copy(out=y_woven[:], in_=y[u][g][:].rearrange("p t m -> p m t"))
+                nc.vector.tensor_copy(
+                    out=y_woven[:].rearrange("p (c i) t -> p c t i", i=4), in_=y[u][g][:].rearrange("p t (c i) -> p c t i", i=4)
+                )
                 nc.vector.quantize_mx(
                     out=y_codes[:].bitcast(FP8X4), scales=y_sc[:, g, cols], in_=y_woven[:].rearrange("p m t -> p (m t)")
                 )
@@ -276,7 +278,8 @@ def tile_list_kinship_closeness_kernel(
         planes(0)
         planes(1)
         for q in range(4):
-            nc.sync.dma_start(
+            queue = nc.sync if q % 2 == 0 else nc.scalar
+            queue.dma_start(
                 out=out_2[:, 4 * q : 4 * q + 4, :].rearrange("g r m -> r g m").bitcast(I32),
                 in_=y_sc[32 * q : 32 * q + 4, :, :].bitcast(I32),
             )

import math
from contextlib import ExitStack

import concourse.mybir as mybir

K, T, S, H, PAIRS, N = 2048, 2048, 1024, 512, 512, 1024
FLOPS = 2 * K * H * S + 2 * H * N * PAIRS

F32 = mybir.dt.float32
BF16 = mybir.dt.bfloat16
I32 = mybir.dt.int32
U32 = mybir.dt.uint32
U16 = mybir.dt.uint16
U8 = mybir.dt.uint8
FP8X4 = mybir.dt.float8_e4m3fn_x4
FP4X4 = mybir.dt.float4_e2m1fn_x4
ALU = mybir.AluOpType
ACT = mybir.ActivationFunctionType

P = 128
PACK = 4
K_PASS = P * PACK
PASSES = K // K_PASS
BANK = 512
GROUPS = N // K_PASS
HALF = PAIRS // 2
THIRD_VECTOR_COLUMNS = 56
LAST_VECTOR_COLUMNS = 48


def tile_list_kinship_closeness_kernel(
    tc, tab_words, tab_scales, offs, pos1, pos2, w1, w2_words, w2_scales, temp, lean, rate, gain, base, out_0, out_1, out_2
):
    nc = tc.nc
    with ExitStack() as ctx:
        keep = ctx.enter_context(tc.tile_pool(name="keep", bufs=1))
        psum = ctx.enter_context(tc.psum_pool(name="psum", bufs=1))

        def sb(shape, dtype, name, tag=None):
            return keep.tile(shape, dtype, name=name, tag=tag or name, align_bytes=64)

        offs_sb = keep.tile([P, S // 16], U16, name="offs_sb")
        pos1_sb = keep.tile([P, PAIRS // 16], U16, name="pos1_sb")
        pos2_sb = keep.tile([P, PAIRS // 16], U16, name="pos2_sb")
        tab = [sb([P, T], U32, f"tab{a}") for a in range(PASSES)]
        raw = [sb([P, PACK, H], F32, f"raw{a}") for a in range(PASSES - 1)]
        raw_last = [sb([P, PACK, H // 2], F32, f"raw_last{u}") for u in range(2)]
        w2_in = sb([P, 2 * N], U8, "w2_in", tag="look0")

        def w1_rows(a):
            return w1[a * K_PASS : (a + 1) * K_PASS, :].rearrange("(p j) c -> p j c", j=PACK)

        tab_sc = sb([P, T], U8, "tab_sc")
        w2_sc_in = sb([P, N], U8, "w2_sc_in")
        nc.gpsimd.memset(tab_sc[:].bitcast(I32), 0)
        for q in range(4):
            nc.gpsimd.dma_start(
                out=tab_sc[32 * q : 32 * q + 16, :].bitcast(I32), in_=tab_scales[:, 4 * q : 4 * q + 4, :].bitcast(I32)
            )
        nc.vector.memset(w2_sc_in[:].bitcast(I32), 0)
        row = {name: sb([P, PACK], F32, name + "_sb") for name in ("temp", "lean", "rate", "gain")}
        base_sb = sb([P, GROUPS, PACK], F32, "base_sb")
        nc.sync.dma_start(offs_sb[:], offs)
        for a in range(PASSES):
            nc.sync.dma_start(out=tab[a][:].bitcast(I32), in_=tab_words[a].rearrange("p t i -> p (t i)").bitcast(I32))
            if a == 1:
                for name, src in (("temp", temp), ("lean", lean), ("rate", rate), ("gain", gain)):
                    nc.sync.dma_start(out=row[name][:], in_=src.rearrange("(p t) -> p t", t=PACK))
                nc.sync.dma_start(out=base_sb[:], in_=base.rearrange("(g p t) -> p g t", g=GROUPS, t=PACK))
            if a < PASSES - 1:
                nc.sync.dma_start(out=raw[a][:], in_=w1_rows(a))
            if a == 1:
                for q in range(4):
                    nc.sync.dma_start(
                        out=w2_sc_in[32 * q : 32 * q + 4, :].bitcast(I32), in_=w2_scales[0, 4 * q : 4 * q + 4, :].bitcast(I32)
                    )
        for u in range(2):
            nc.sync.dma_start(out=raw_last[u][:], in_=w1_rows(PASSES - 1)[:, :, u * (H // 2) : (u + 1) * (H // 2)])
        nc.sync.dma_start(pos1_sb[:], pos1)
        nc.sync.dma_start(pos2_sb[:], pos2)
        nc.sync.dma_start(out=w2_in[:].bitcast(I32), in_=w2_words[0].bitcast(I32))

        def small(name, width=PACK):
            return sb([P, width], F32, name)

        step, sign, size, size2, root, root2, neg_root = [small(n) for n in ("step", "sign", "size", "size2", "root", "root2", "neg_root")]
        half_power, rate_quarter, turn, neg_temp = [small(n) for n in ("half_power", "rate_quarter", "turn", "neg_temp")]
        one, shift = small("one", 1), small("shift", 1)
        nc.gpsimd.memset(half_power[:], 0.5)
        nc.gpsimd.memset(one[:], 1.0)
        nc.gpsimd.tensor_scalar(shift[:], one[:], -math.pi / 8.0, 0.0, ALU.mult, ALU.add)
        nc.gpsimd.tensor_scalar(neg_temp[:], row["temp"][:], -1.0, 0.0, ALU.mult, ALU.add)
        nc.gpsimd.tensor_scalar(step[:], row["gain"][:], 0.0, None, ALU.is_ge)
        nc.gpsimd.tensor_scalar(sign[:], step[:], 2.0, -1.0, ALU.mult, ALU.add)
        nc.gpsimd.tensor_tensor(size[:], row["gain"][:], sign[:], ALU.mult)
        nc.gpsimd.tensor_scalar(size2[:], size[:], 2.0, 0.0, ALU.mult, ALU.add)
        nc.gpsimd.tensor_tensor(root[:], size2[:], half_power[:], ALU.pow)
        nc.gpsimd.tensor_scalar(root2[:], root[:], 2.0, 0.0, ALU.mult, ALU.add)
        nc.gpsimd.tensor_scalar(neg_root[:], root[:], -1.0, 0.0, ALU.mult, ALU.add)
        nc.gpsimd.tensor_scalar(rate_quarter[:], row["rate"][:], 0.25, 0.0, ALU.mult, ALU.add)
        nc.gpsimd.tensor_tensor(turn[:], rate_quarter[:], sign[:], ALU.mult)

        w2_sc = sb([P, N], U8, "w2_sc")
        nc.gpsimd.tensor_copy(
            out=w2_sc[:].rearrange("p (g t q) -> p g t q", g=GROUPS, t=PACK),
            in_=w2_sc_in[:].rearrange("p (g q t) -> p g t q", g=GROUPS, t=PACK),
        )

        v_words = [sb([P, S], U32, f"v_words{a}") for a in range(PASSES)]
        v_sc = sb([P, S], U8, "v_sc")
        w_bf = [sb([P, PACK, P, PACK], BF16, f"w_bf{a}") for a in range(PASSES)]
        w_codes = [sb([P, H], U32, f"w_codes{a}") for a in range(PASSES)]
        w_sc = [sb([P, H], U8, f"w_sc{a}") for a in range(PASSES)]
        h_ps = [[psum.tile([P, BANK], F32, name=f"h_ps{t}{u}", tag=f"bank{2 * t + u}") for u in range(2)] for t in range(PACK)]

        def dealt(a, src, m0, m1, first):
            dst = w_bf[a][:, :, m0:m1, :].rearrange("p t m j -> p m j t")
            view = src[:].rearrange("p j (m t) -> p m j t", t=PACK)[:, m0 - first : m1 - first, :, :]
            return dst, view

        def quantize_w(a, t0, t1):
            nc.vector.quantize_mx(
                out=w_codes[a][:, t0 * P : t1 * P].bitcast(FP8X4),
                scales=w_sc[a][:, t0 * P : t1 * P],
                in_=w_bf[a][:, t0:t1, :, :].rearrange("p t m j -> p (t m j)"),
            )

        def first_matmuls(a, t):
            for u in range(2):
                cols = slice(u * BANK, (u + 1) * BANK)
                nc.tensor.matmul_mx(
                    out=h_ps[t][u][:],
                    lhsT=w_codes[a][:, t * P : (t + 1) * P].bitcast(FP8X4),
                    lhsT_scale=w_sc[a][:, t * P : (t + 1) * P],
                    rhs=v_words[a][:, cols].bitcast(FP8X4),
                    rhs_scale=v_sc[4 * a : P, cols],
                    start=(a == 0),
                    stop=(a == PASSES - 1),
                )

        for a in range(PASSES):
            nc.vector.tensor_copy(out=v_words[a][:], in_=tab[a][:].indirect(offs_sb[:]))
            if a == 0:
                nc.vector.tensor_copy(out=v_sc[:], in_=tab_sc[:].indirect(offs_sb[:]))
            if a < PASSES - 1:
                share = THIRD_VECTOR_COLUMNS if a == 2 else 0
                dst, view = dealt(a, raw[a], share, P, 0)
                nc.scalar.activation(out=dst, in_=view, func=ACT.Copy)
                if share:
                    dst, view = dealt(a, raw[a], 0, share, 0)
                    nc.vector.tensor_copy(out=dst, in_=view)
                quantize_w(a, 0, PACK)
                for t in range(PACK):
                    first_matmuls(a, t)
        last = PASSES - 1
        mid = P // 2
        cut = mid + LAST_VECTOR_COLUMNS
        dst, view = dealt(last, raw_last[0], 0, mid, 0)
        nc.scalar.activation(out=dst, in_=view, func=ACT.Copy)
        dst, view = dealt(last, raw_last[1], mid, cut, mid)
        nc.vector.tensor_copy(out=dst, in_=view)
        dst, view = dealt(last, raw_last[1], cut, P, mid)
        nc.scalar.activation(out=dst, in_=view, func=ACT.Copy)
        for t in range(PACK):
            quantize_w(last, t, t + 1)
            first_matmuls(last, t)

        w2_dealt = sb([P, 2 * N], U8, "w2_dealt")
        nc.scalar.copy(
            out=w2_dealt[:].bitcast(U16).rearrange("p (g t q) -> p g t q", g=GROUPS, t=PACK),
            in_=w2_in[:].bitcast(U16).rearrange("p (g q t) -> p g t q", g=GROUPS, t=PACK),
        )

        h = [sb([P, S], F32, f"h{t}") for t in range(PACK)]
        peak = [sb([P, 2], F32, f"peak{t}") for t in range(PACK)]
        look_bias = sb([P, PACK], F32, "look_bias", tag="sine00")
        look = [sb([P, PAIRS], F32, f"look{t}") for t in range(PACK)]
        pick = [sb([P, PAIRS], F32, f"pick{t}") for t in range(PACK)]
        for t in range(PACK):
            for u in range(2):
                nc.vector.tensor_scalar(
                    h[t][:, u * BANK : (u + 1) * BANK], h_ps[t][u][:], 1.0, None, ALU.mult, ALU.max, accum_out=peak[t][:, u : u + 1]
                )
            nc.gpsimd.tensor_scalar(
                look_bias[:, t : t + 1], peak[t][:, 0:1], peak[t][:, 1:2], neg_temp[:, t : t + 1], ALU.max, ALU.mult
            )
            nc.scalar.activation(
                out=look[t][:],
                in_=h[t][:].indirect(pos1_sb[:]),
                func=ACT.Exp,
                bias=look_bias[:, t : t + 1],
                scale=row["temp"][:, t : t + 1],
            )
        for t in range(PACK):
            nc.vector.tensor_copy(out=pick[t][:], in_=h[t][:].indirect(pos2_sb[:]))
        larger = look
        gained = sb([P, PACK, PAIRS], F32, "gained")
        for t in range(PACK):
            nc.vector.scalar_tensor_tensor(larger[t][:], look[t][:], row["lean"][:, t : t + 1], pick[t][:], ALU.mult, ALU.max)
        for t in range(PACK):
            nc.vector.tensor_scalar(
                gained[:, t, :], larger[t][:], row["gain"][:, t : t + 1], size[:, t : t + 1], ALU.mult, ALU.subtract
            )

        wave = [sb([P, PACK, HALF], F32, f"wave{u}") for u in range(2)]
        for u in range(2):
            cols = slice(u * HALF, (u + 1) * HALF)
            sine = [sb([P, HALF], F32, f"sine{u}{t}") for t in range(PACK)]
            square = [sb([P, HALF], F32, f"square{u}{t}") for t in range(PACK)]
            for t in range(PACK):
                nc.scalar.activation(out=sine[t][:], in_=pick[t][:, cols], func=ACT.Sin, scale=turn[:, t : t + 1], bias=shift[:])
            for t in range(PACK):
                nc.scalar.activation(out=square[t][:], in_=sine[t][:], func=ACT.Square)
            for t in range(PACK):
                nc.scalar.activation(
                    out=wave[u][:, t, :], in_=square[t][:], func=ACT.Square, scale=root2[:, t : t + 1], bias=neg_root[:, t : t + 1]
                )

        z_codes = [sb([P, HALF], U32, f"z_codes{u}") for u in range(2)]
        z_sc = [sb([P, HALF], U8, f"z_sc{u}") for u in range(2)]
        y = [[sb([P, PACK, HALF], F32, f"y{u}{g}") for g in range(GROUPS)] for u in range(2)]
        y_sc = sb([P, GROUPS, PAIRS], U8, "y_sc")

        def make_z(u):
            cols = slice(u * HALF, (u + 1) * HALF)
            z_woven = sb([P, HALF, PACK], BF16, f"z_woven{u}")
            nc.vector.tensor_tensor(
                z_woven[:].rearrange("p (c i) t -> p c t i", i=4),
                gained[:, :, cols].rearrange("p t (c i) -> p c t i", i=4),
                wave[u][:].rearrange("p t (c i) -> p c t i", i=4),
                ALU.add,
            )
            return z_woven

        def second_stage(u, z_woven):
            cols = slice(u * HALF, (u + 1) * HALF)
            nc.vector.quantize_mx(out=z_codes[u][:].bitcast(FP8X4), scales=z_sc[u][:], in_=z_woven[:].rearrange("p m t -> p (m t)"))
            for g in range(GROUPS):
                for pair in range(2):
                    bank = 4 * u + 2 * g + pair
                    y_ps = psum.tile([P, 2, HALF], F32, name=f"y_ps{bank}", tag=f"bank{bank}")
                    for e in range(2):
                        col = (g * PACK + 2 * pair + e) * P
                        nc.tensor.matmul_mx(
                            out=y_ps[:, e, :],
                            lhsT=w2_dealt[:, 2 * col : 2 * (col + P)].bitcast(FP4X4),
                            lhsT_scale=w2_sc[:, col : col + P],
                            rhs=z_codes[u][:].bitcast(FP8X4),
                            rhs_scale=z_sc[u][:],
                            start=True,
                            stop=True,
                        )
                    for e in range(2):
                        t = 2 * pair + e
                        nc.scalar.activation(out=y[u][g][:, t, :], in_=y_ps[:, e, :], func=ACT.Identity, bias=base_sb[:, g, t : t + 1])
                rows = out_0[g * K_PASS : (g + 1) * K_PASS, cols].rearrange("(p t) m -> p t m", t=PACK)
                nc.sync.dma_start(out=rows, in_=y[u][g][:])

        def planes(u):
            cols = slice(u * HALF, (u + 1) * HALF)
            for g in range(GROUPS):
                y_woven = sb([P, HALF, PACK], BF16, f"y_woven{u}{g}")
                y_codes = sb([P, HALF], U32, f"y_codes{u}{g}")
                nc.vector.tensor_copy(
                    out=y_woven[:].rearrange("p (c i) t -> p c t i", i=4), in_=y[u][g][:].rearrange("p t (c i) -> p c t i", i=4)
                )
                nc.vector.quantize_mx(
                    out=y_codes[:].bitcast(FP8X4), scales=y_sc[:, g, cols], in_=y_woven[:].rearrange("p m t -> p (m t)")
                )
                nc.sync.dma_start(
                    out=out_1[g, :, cols, :].rearrange("p m t -> p (m t)").bitcast(I32), in_=y_codes[:].bitcast(I32)
                )

        woven = [make_z(0)]
        second_stage(0, woven[0])
        woven.append(make_z(1))
        second_stage(1, woven[1])
        planes(0)
        planes(1)
        for q in range(4):
            queue = nc.sync if q % 2 == 0 else nc.scalar
            queue.dma_start(
                out=out_2[:, 4 * q : 4 * q + 4, :].rearrange("g r m -> r g m").bitcast(I32),
                in_=y_sc[32 * q : 32 * q + 4, :, :].bitcast(I32),
            )
